import numpy as np
import ml_dtypes


def mxq(x, axis, fmt="e4m3"):
    dtype, down = {"e4m3": (ml_dtypes.float8_e4m3fn, 7), "e5m2": (ml_dtypes.float8_e5m2, 14)}[fmt]
    v = np.moveaxis(np.asarray(x, np.float32).astype(ml_dtypes.bfloat16).astype(np.float64), axis, -1)
    blocks = v.reshape(v.shape[:-1] + (-1, 32))
    amax = np.abs(blocks).max(-1, keepdims=True)
    byte = np.maximum(np.where(amax > 0, np.frexp(amax)[1] - 1 + 127, 0) - down, 1)
    scale = np.exp2(byte - 127.0)
    codes = (blocks / scale).astype(np.float32).astype(dtype).astype(np.float64)
    return np.moveaxis((codes * scale).reshape(v.shape), -1, axis)


WIDE = False


def mx_kscale(k):
    if not WIDE:
        return np.ones(k)
    levels = np.array([10, -10, 5, -5, 0])
    if k % 512:
        return np.exp2(np.random.permutation(np.resize(levels, k // 32))).repeat(32)
    a = np.empty((k // 512, 16))
    for p in range(k // 512):
        a[p, :8] = np.random.permutation(np.resize(levels, 8))
        for g in range(8):
            far = levels[np.abs(levels - a[p, g]) >= 10]
            a[p, g + 8] = far[np.random.randint(len(far))]
    return np.exp2(a.ravel()).repeat(32)


def f64(x):
    return np.asarray(x).astype(np.float64)


def striped(idx):
    return np.tile(np.asarray(idx).reshape(-1, 16).T, (8, 1)).astype(np.uint16)


def unstriped(offs):
    return offs[:16].T.reshape(-1).astype(np.int64)


def striped8(idx):
    return np.asarray(idx).reshape(8, -1, 16).transpose(0, 2, 1).reshape(128, -1).astype(np.uint16)


def unstriped8(offs):
    return offs.reshape(8, 16, -1).transpose(0, 2, 1).reshape(8, -1).astype(np.int64)


def pick8(x, idx, run):
    r = np.arange(len(x))
    return x[r[:, None], idx[r % (8 * run) // run]]


E2M1 = np.array([0.0, 0.5, 1.0, 1.5, 2.0, 3.0, 4.0, 6.0, -0.0, -0.5, -1.0, -1.5, -2.0, -3.0, -4.0, -6.0])


def pack_weight(w, fmt):
    k, n = w.shape
    w = f64(np.asarray(w, np.float32).astype(ml_dtypes.bfloat16)).reshape(k // 32, 32, n)
    amax = np.abs(w).max(1)
    if fmt == "e4m3":
        byte = np.frexp(amax)[1] - 1 + 127 - 7
    else:
        mant, ex = np.frexp(amax / 6.0)
        byte = np.where(mant > 0.5, ex, ex - 1) + 127
    byte = np.clip(np.where(amax > 0, byte, 1), 1, 254)
    scaled = (w * np.exp2(127.0 - byte)[:, None, :]).reshape(k, n).astype(np.float32)
    by_word = np.ascontiguousarray(scaled.reshape(k // 512, 128, 4, n).transpose(0, 1, 3, 2))
    if fmt == "e4m3":
        words = by_word.astype(ml_dtypes.float8_e4m3fn).view(np.uint8)
    else:
        c = by_word.astype(ml_dtypes.float4_e2m1fn).view(np.uint8) & 0xF
        words = (c[..., 0::2] | (c[..., 1::2] << 4)).reshape(k // 512, 128, 2 * n)
    return np.ascontiguousarray(words), np.ascontiguousarray(byte.astype(np.uint8).reshape(k // 512, 16, n))


def unpack_weight(words, scales, fmt):
    g, _, n = scales.shape
    words = np.ascontiguousarray(words).reshape(g, 128, n, -1)
    if fmt == "e4m3":
        vals = words.view(ml_dtypes.float8_e4m3fn).astype(np.float64)
    else:
        nib = np.empty((g, 128, n, 4), np.uint8)
        nib[..., 0::2] = words & 0xF
        nib[..., 1::2] = words >> 4
        vals = E2M1[nib]
    vals = vals * np.repeat(np.exp2(scales.astype(np.float64) - 127.0), 8, axis=1)[..., None]
    return vals.transpose(0, 1, 3, 2).reshape(g * 512, n)


K, J, R, T, F, C, O, N, U = 512, 1024, 512, 2048, 1024, 2048, 512, 256, 256


def setup_inputs():
    n = np.random.standard_normal
    idx = np.random.permutation(T)[:J]
    idx2 = np.stack([np.random.permutation(F)[:R] for _ in range(8)])
    idx3 = np.random.permutation(C)[:J]
    idx4 = np.random.permutation(C)[:O]
    idx5 = np.stack([np.random.permutation(C)[:O] for _ in range(8)])
    idx6 = np.stack([np.random.permutation(O)[:U] for _ in range(8)])
    idx7 = np.stack([np.random.permutation(O)[:U] for _ in range(8)])
    fk = mx_kscale(K)
    fr = mx_kscale(R)
    xtp = pack_weight(n((K, T)) * fk[:, None], "e4m3")
    wbp = pack_weight(n((R, N)) * 1 / np.sqrt(R) / fr[:, None], "e2m1")
    wop = pack_weight(n((R, N)) * 1 / np.sqrt(R) / fr[:, None], "e4m3")
    return {
        "xt_words": xtp[0],
        "xt_scales": xtp[1],
        "ua": (np.random.randint(-7, 8, (K, F)).astype(np.float64)).astype(np.float32),
        "ha": ((np.random.randint(8, 25, (K, 1)) / 1024.0) / fk[:, None]).astype(np.float32),
        "sa": (np.random.uniform(0.5, 1.6, (R, 1)) * fr[:, None]).astype(np.float32),
        "sb": (np.random.uniform(0.5, 1.6, (R, 1)) * fr[:, None]).astype(np.float32),
        "wb_words": wbp[0],
        "wb_scales": wbp[1],
        "wo_words": wop[0],
        "wo_scales": wop[1],
        "so": (np.random.uniform(0.5, 1.6, (N, 1))).astype(np.float32),
        "sp": (np.random.uniform(0.5, 1.6, (N, 1))).astype(np.float32),
        "offs": striped(idx),
        "offs2": striped8(idx2),
        "offs3": striped(idx3),
        "offs4": striped(idx4),
        "offs5": striped8(idx5),
        "offs6": striped8(idx6),
        "offs7": striped8(idx7),
    }


def reference(xt_words, xt_scales, ua, ha, sa, sb, wb_words, wb_scales, wo_words, wo_scales, so, sp, offs, offs2, offs3, offs4, offs5, offs6, offs7):
    idx = unstriped(offs)
    idx2 = unstriped8(offs2)
    idx3 = unstriped(offs3)
    idx4 = unstriped(offs4)
    idx5 = unstriped8(offs5)
    idx6 = unstriped8(offs6)
    idx7 = unstriped8(offs7)
    xtu = unpack_weight(xt_words, xt_scales, "e4m3")
    wbu = unpack_weight(wb_words, wb_scales, "e2m1")
    wou = unpack_weight(wo_words, wo_scales, "e4m3")
    wc = pick8(f64(ua), idx2, 64) * f64(ha)
    wcq = mxq(wc, 0, "e4m3")
    xtidxg = xtu[:, idx]
    a = wcq.T @ xtidxg
    pw = np.zeros((R, C))
    pw[:, idx3] = a
    hid = np.abs(pw[:, idx4] * f64(sa) - pick8(pw, idx5, 64) * f64(sb))
    hidq = mxq(hid, 0, "e4m3")
    p = wbu.T @ hidq
    q = wou.T @ hidq
    y = pick8(p, idx6, 16) * f64(so) - pick8(q, idx7, 16) * f64(sp)
    return y

@@ -1,0 +1,225 @@
+from contextlib import ExitStack
+
+import concourse.mybir as mybir
+
+F32 = mybir.dt.float32
+BF16 = mybir.dt.bfloat16
+I32 = mybir.dt.int32
+U32 = mybir.dt.uint32
+U16 = mybir.dt.uint16
+U8 = mybir.dt.uint8
+FP8X4 = mybir.dt.float8_e4m3fn_x4
+FP4X4 = mybir.dt.float4_e2m1fn_x4
+ACT = mybir.ActivationFunctionType
+ALU = mybir.AluOpType
+
+K, J, R, T, F, C, O, N, U = 512, 1024, 512, 2048, 1024, 2048, 512, 256, 256
+P = 128
+PACK = 4
+HALF = 512
+OH = O // 2
+FLOPS = 2 * K * R * J + 2 * 2 * R * N * O
+
+
+def tile_picked_tokens_codes_one_boardmixed_outcomes_outmeet_kernel(
+    tc, xt_words, xt_scales, ua, ha, sa, sb, wb_words, wb_scales, wo_words, wo_scales, so, sp,
+    offs, offs2, offs3, offs4, offs5, offs6, offs7, out,
+):
+    nc = tc.nc
+    with ExitStack() as ctx:
+        lists = ctx.enter_context(tc.tile_pool(name="lists", bufs=1))
+        keep = ctx.enter_context(tc.tile_pool(name="keep", bufs=1))
+        psum = ctx.enter_context(tc.psum_pool(name="psum", bufs=1))
+
+        def load_list(src, name):
+            tile = lists.tile([P, src.shape[1]], U16, name=name)
+            nc.sync.dma_start(tile[:], src)
+            return tile
+
+        def entries(tile, lo, hi):
+            return tile[:, lo // 16 : hi // 16]
+
+        def load_by_word(src, name):
+            tile = keep.tile([P, PACK], F32, name=name)
+            nc.sync.dma_start(tile[:], src.rearrange("(p t) o -> p (t o)", t=PACK))
+            return tile
+
+        ha_sb = keep.tile([P, PACK], F32, name="ha_sb")
+        nc.scalar.dma_start(ha_sb[:], ha.rearrange("(p t) o -> p (t o)", t=PACK))
+        xs_win = keep.tile([P, T], U8, name="xs_win")
+        nc.vector.memset(xs_win[:].bitcast(I32), 0)
+        for q in range(4):
+            nc.scalar.dma_start(xs_win[:].bitcast(I32)[32 * q : 32 * q + 4, :], xt_scales[0].bitcast(I32)[4 * q : 4 * q + 4, :])
+        l_ua = load_list(offs2, "l_ua")
+        ua_rows = ua.rearrange("(p t) f -> t p f", t=PACK)
+        ua_sb = [keep.tile([P, F], F32, name=f"ua{t}") for t in range(PACK)]
+        nc.sync.dma_start(ua_sb[0][:], ua_rows[0])
+        l_xt = load_list(offs, "l_xt")
+        for t in range(1, PACK):
+            nc.sync.dma_start(ua_sb[t][:], ua_rows[t])
+        xw_win = keep.tile([P, T], U32, name="xw_win")
+        nc.sync.dma_start(xw_win[:].bitcast(I32), xt_words[0].rearrange("p n t -> p (n t)").bitcast(I32))
+        l_put = load_list(offs3, "l_put")
+        l_a = load_list(offs4, "l_a")
+        l_b = load_list(offs5, "l_b")
+        sa_sb = load_by_word(sa, "sa_sb")
+        sb_sb = load_by_word(sb, "sb_sb")
+
+        board = [keep.tile([P, C], F32, name=f"board{t}") for t in range(PACK)]
+        for t in range(PACK):
+            nc.vector.memset(board[t][:].bitcast(I32), 0)
+        xs = keep.tile([P, J], U8, name="xs", align_bytes=64)
+        nc.vector.tensor_copy(out=xs[:], in_=xs_win[:].indirect(l_xt[:]))
+
+        wb_w = keep.tile([P, 2 * N], U8, name="wb_w", align_bytes=64)
+        wo_w = keep.tile([P, N], U32, name="wo_w", align_bytes=64)
+        wb_s = keep.tile([P, N], U8, name="wb_s", align_bytes=64)
+        wo_s = keep.tile([P, N], U8, name="wo_s", align_bytes=64)
+        nc.sync.dma_start(wb_w[:].bitcast(I32), wb_words[0].bitcast(I32))
+        nc.sync.dma_start(wo_w[:].bitcast(I32), wo_words[0].rearrange("p n t -> p (n t)").bitcast(I32))
+        for plane, src in ((wb_s, wb_scales), (wo_s, wo_scales)):
+            nc.vector.memset(plane[:].bitcast(I32), 0)
+            for q in range(4):
+                nc.sync.dma_start(plane[:].bitcast(I32)[32 * q : 32 * q + 4, :], src[0].bitcast(I32)[4 * q : 4 * q + 4, :])
+        l_p = load_list(offs6, "l_p")
+        l_q = load_list(offs7, "l_q")
+        so_sb = [keep.tile([P, 1], F32, name=f"so{u}") for u in range(2)]
+        sp_sb = [keep.tile([P, 1], F32, name=f"sp{u}") for u in range(2)]
+        for u in range(2):
+            nc.sync.dma_start(so_sb[u][:], so[P * u : P * (u + 1), :])
+            nc.sync.dma_start(sp_sb[u][:], sp[P * u : P * (u + 1), :])
+
+        wc = keep.tile([P, PACK, R], BF16, name="wc")
+        for j in range(PACK):
+            nc.scalar.activation(out=wc[:, j, :], in_=ua_sb[j][:].indirect(l_ua[:]), func=ACT.Copy, scale=ha_sb[:, j : j + 1])
+        wc_dealt = wc[:].rearrange("p j (m t) -> p t m j", t=PACK)
+        wc_w = keep.tile([P, R], U32, name="wc_w", align_bytes=64)
+        wc_s = keep.tile([P, R], U8, name="wc_s", align_bytes=64)
+        wc_g = keep.tile([P, PACK, P, PACK], BF16, name="wc_g", align_bytes=64)
+
+        def quantize_wc(lo, hi):
+            cols = slice(lo * P, hi * P)
+            nc.vector.quantize_mx(out=wc_w[:, cols].bitcast(FP8X4), scales=wc_s[:, cols], in_=wc_g[:, lo:hi].rearrange("p t m j -> p (t m j)"))
+
+        nc.vector.tensor_copy(out=wc_g[:, 0], in_=wc_dealt[:, 0])
+        nc.scalar.copy(out=wc_g[:, 1:PACK], in_=wc_dealt[:, 1:PACK])
+        xw = keep.tile([P, J], U32, name="xw", align_bytes=64)
+
+        def gather_words(lo, hi):
+            nc.vector.tensor_copy(out=xw[:, lo:hi], in_=xw_win[:].indirect(entries(l_xt, lo, hi)))
+
+        quantize_wc(0, 1)
+        gather_words(0, 256)
+        gather_words(256, HALF)
+        quantize_wc(1, PACK)
+        gather_words(HALF, J)
+
+        acc = {}
+        for t in range(PACK):
+            for h in range(2):
+                acc[t, h] = psum.tile([P, HALF], F32, name=f"acc{t}{h}", tag=f"bank{2 * t + h}")
+
+        def product(t, lo, hi):
+            nc.tensor.matmul_mx(
+                out=acc[t, lo // HALF][:, lo % HALF : lo % HALF + hi - lo], lhsT=wc_w[:, t * P : (t + 1) * P].bitcast(FP8X4), lhsT_scale=wc_s[:, t * P : (t + 1) * P],
+                rhs=xw[:, lo:hi].bitcast(FP8X4), rhs_scale=xs[:, lo:hi], start=True, stop=True,
+            )
+
+        a_sb = [keep.tile([P, J], F32, name=f"a{t}") for t in range(PACK)]
+
+        def fetch_scalar(t, lo, hi):
+            nc.scalar.copy(out=a_sb[t][:, lo:hi], in_=acc[t, lo // HALF][:, lo % HALF : lo % HALF + hi - lo])
+
+        def fetch_vector(t, lo, hi):
+            nc.vector.tensor_copy(out=a_sb[t][:, lo:hi], in_=acc[t, lo // HALF][:, lo % HALF : lo % HALF + hi - lo])
+
+        def put_scalar(t, lo, hi):
+            nc.scalar.activation(out=board[t][:].indirect(entries(l_put, lo, hi)), in_=a_sb[t][:, lo:hi], func=ACT.Copy)
+
+        def put_vector(t, lo, hi):
+            nc.vector.tensor_copy(out=board[t][:].indirect(entries(l_put, lo, hi)), in_=a_sb[t][:, lo:hi])
+
+        first = [keep.tile([P, O], F32, name=f"first{t}") for t in range(PACK)]
+        second = [keep.tile([P, O], F32, name=f"second{t}") for t in range(PACK)]
+        diff = keep.tile([P, PACK, O], F32, name="diff")
+
+        def read_second(t):
+            nc.scalar.activation(out=second[t][:], in_=board[t][:].indirect(l_b[:]), func=ACT.Copy, scale=sb_sb[:, t : t + 1])
+
+        def read_first(t, lo, hi):
+            nc.scalar.activation(out=first[t][:, lo:hi], in_=board[t][:].indirect(entries(l_a, lo, hi)), func=ACT.Copy, scale=sa_sb[:, t : t + 1])
+
+        def subtract(t, lo, hi):
+            nc.vector.tensor_tensor(out=diff[:, t, lo:hi], in0=first[t][:, lo:hi], in1=second[t][:, lo:hi], op=ALU.subtract)
+
+        product(0, 0, 256)
+        fetch_scalar(0, 0, 256)
+        put_scalar(0, 0, 256)
+        product(1, 0, HALF)
+        product(0, 256, HALF)
+        product(0, HALF, J)
+        product(1, HALF, J)
+        for t in (2, 3):
+            product(t, 0, HALF)
+            product(t, HALF, J)
+        fetch_vector(1, 0, HALF)
+        put_vector(1, 0, HALF)
+        fetch_vector(1, HALF, J)
+        put_vector(1, HALF, J)
+        fetch_scalar(0, 256, HALF)
+        fetch_scalar(0, HALF, J)
+        put_scalar(0, 256, 640)
+        fetch_scalar(2, 0, HALF)
+        fetch_scalar(2, HALF, J)
+        put_scalar(0, 640, J)
+        put_vector(2, 0, J)
+        fetch_scalar(3, 0, HALF)
+        put_scalar(3, 0, 384)
+        fetch_vector(3, HALF, J)
+        put_vector(3, 384, J)
+        for t in range(3):
+            read_second(t)
+            read_first(t, 0, O)
+        read_second(3)
+        read_first(3, 0, OH)
+        read_first(3, OH, O)
+        for t in range(3):
+            subtract(t, 0, O)
+        subtract(3, 0, OH)
+        subtract(3, OH, O)
+
+        hid_g = [keep.tile([P, OH, PACK], BF16, name=f"hid_g{h}", align_bytes=64) for h in range(2)]
+        hid_w = keep.tile([P, O], U32, name="hid_w", align_bytes=64)
+        hid_s = keep.tile([P, O], U8, name="hid_s", align_bytes=64)
+        nc.scalar.activation(out=hid_g[1][:], in_=diff[:, :, OH:O].rearrange("p t o -> p o t"), func=ACT.Abs)
+        low = diff[:, :, 0:OH].rearrange("p t o -> p o t")
+        nc.vector.scalar_tensor_tensor(out=hid_g[0][:], in0=low, scalar=-1.0, in1=low, op0=ALU.mult, op1=ALU.max)
+        for h in range(2):
+            cols = slice(h * OH, (h + 1) * OH)
+            nc.vector.quantize_mx(out=hid_w[:, cols].bitcast(FP8X4), scales=hid_s[:, cols], in_=hid_g[h][:].rearrange("p o t -> p (o t)"))
+
+        outcome = {(m, u): keep.tile([P, O], F32, name=f"outcome{m}{u}") for m in range(2) for u in range(2)}
+
+        def second_product(m, u, lo, hi, tag, copy):
+            bank = psum.tile([P, hi - lo], F32, name=f"res{tag}", tag=f"bank{tag}")
+            cols = slice(u * P, (u + 1) * P)
+            if m == 0:
+                w, s = wb_w[:, 2 * u * P : 2 * (u + 1) * P].bitcast(FP4X4), wb_s[:, cols]
+            else:
+                w, s = wo_w[:, cols].bitcast(FP8X4), wo_s[:, cols]
+            nc.tensor.matmul_mx(out=bank[:], lhsT=w, lhsT_scale=s, rhs=hid_w[:, lo:hi].bitcast(FP8X4), rhs_scale=hid_s[:, lo:hi], start=True, stop=True)
+            copy(out=outcome[m, u][:, lo:hi], in_=bank[:])
+
+        second_product(0, 0, 0, OH, 0, nc.scalar.copy)
+        second_product(0, 0, OH, O, 1, nc.scalar.copy)
+        second_product(1, 0, 0, O, 2, nc.vector.tensor_copy)
+        second_product(0, 1, 0, O, 3, nc.vector.tensor_copy)
+        second_product(1, 1, 0, O, 4, nc.vector.tensor_copy)
+        for u in range(2):
+            p_at = keep.tile([P, U], F32, name=f"p_at{u}")
+            q_at = keep.tile([P, U], F32, name=f"q_at{u}")
+            y = keep.tile([P, U], F32, name=f"y{u}")
+            nc.scalar.activation(out=p_at[:], in_=outcome[0, u][:].indirect(l_p[:]), func=ACT.Copy, scale=so_sb[u][:])
+            nc.scalar.activation(out=q_at[:], in_=outcome[1, u][:].indirect(l_q[:]), func=ACT.Copy, scale=sp_sb[u][:])
+            nc.vector.tensor_tensor(out=y[:], in0=p_at[:], in1=q_at[:], op=ALU.subtract)
+            nc.sync.dma_start(out[u * P : (u + 1) * P, :], y[:])

@@ -50,6 +50,9 @@ def tile_picked_tokens_codes_one_boardmixed_outcomes_outmeet_kernel(
         nc.vector.memset(xs_win[:].bitcast(I32), 0)
         for q in range(4):
             nc.scalar.dma_start(xs_win[:].bitcast(I32)[32 * q : 32 * q + 4, :], xt_scales[0].bitcast(I32)[4 * q : 4 * q + 4, :])
+        idle = keep.tile([P, 16], F32, name="idle")
+        nc.gpsimd.memset(idle[:, 0:1], 0.0)
+        nc.scalar.activation(out=idle[:, 8:9], in_=idle[:, 0:1], func=ACT.Copy)
         l_ua = load_list(offs2, "l_ua")
         ua_rows = ua.rearrange("(p t) f -> t p f", t=PACK)
         ua_sb = [keep.tile([P, F], F32, name=f"ua{t}") for t in range(PACK)]

@@ -69,8 +69,9 @@ def tile_picked_tokens_codes_one_boardmixed_outcomes_outmeet_kernel(
         sb_sb = load_by_word(sb, "sb_sb")
 
         board = [keep.tile([P, C], F32, name=f"board{t}") for t in range(PACK)]
-        for t in range(PACK):
+        for t in range(2):
             nc.vector.memset(board[t][:].bitcast(I32), 0)
+            nc.gpsimd.memset(board[t + 2][:].bitcast(I32), 0)
         xs = keep.tile([P, J], U8, name="xs", align_bytes=64)
         nc.vector.tensor_copy(out=xs[:], in_=xs_win[:].indirect(l_xt[:]))
 
@@ -105,14 +106,17 @@ def tile_picked_tokens_codes_one_boardmixed_outcomes_outmeet_kernel(
             nc.vector.quantize_mx(out=wc_w[:, cols].bitcast(FP8X4), scales=wc_s[:, cols], in_=wc_g[:, lo:hi].rearrange("p t m j -> p (t m j)"))
 
         nc.vector.tensor_copy(out=wc_g[:, 0], in_=wc_dealt[:, 0])
-        nc.scalar.copy(out=wc_g[:, 1:PACK], in_=wc_dealt[:, 1:PACK])
+        nc.scalar.copy(
+            out=wc_g[:].rearrange("p t (c i) j -> p c t i j", i=2)[:, :, 1:PACK],
+            in_=wc[:].rearrange("p j (c i t) -> p c t i j", i=2, t=PACK)[:, :, 1:PACK],
+        )
         xw = keep.tile([P, J], U32, name="xw", align_bytes=64)
 
         def gather_words(lo, hi):
             nc.vector.tensor_copy(out=xw[:, lo:hi], in_=xw_win[:].indirect(entries(l_xt, lo, hi)))
 
-        quantize_wc(0, 1)
         gather_words(0, 256)
+        quantize_wc(0, 1)
         gather_words(256, HALF)
         quantize_wc(1, PACK)
         gather_words(HALF, J)
@@ -145,6 +149,11 @@ def tile_picked_tokens_codes_one_boardmixed_outcomes_outmeet_kernel(
         first = [keep.tile([P, O], F32, name=f"first{t}") for t in range(PACK)]
         second = [keep.tile([P, O], F32, name=f"second{t}") for t in range(PACK)]
         diff = keep.tile([P, PACK, O], F32, name="diff")
+        mag = keep.tile([P, PACK, OH], BF16, name="mag")
+
+        def magnitude(t):
+            d = diff[:, t, 0:OH]
+            nc.vector.scalar_tensor_tensor(out=mag[:, t, :], in0=d, scalar=-1.0, in1=d, op0=ALU.mult, op1=ALU.max)
 
         def read_second(t):
             nc.scalar.activation(out=second[t][:], in_=board[t][:].indirect(l_b[:]), func=ACT.Copy, scale=sb_sb[:, t : t + 1])
@@ -184,20 +193,31 @@ def tile_picked_tokens_codes_one_boardmixed_outcomes_outmeet_kernel(
             read_second(t)
             read_first(t, 0, O)
         read_second(3)
-        read_first(3, 0, OH)
         read_first(3, OH, O)
-        for t in range(3):
-            subtract(t, 0, O)
-        subtract(3, 0, OH)
+        read_first(3, 0, OH)
+        subtract(0, 0, O)
+        subtract(1, 0, O)
+        magnitude(0)
+        subtract(2, 0, O)
+        magnitude(1)
+        magnitude(2)
         subtract(3, OH, O)
+        subtract(3, 0, OH)
+        magnitude(3)
 
         hid_g = [keep.tile([P, OH, PACK], BF16, name=f"hid_g{h}", align_bytes=64) for h in range(2)]
         hid_w = keep.tile([P, O], U32, name="hid_w", align_bytes=64)
         hid_s = keep.tile([P, O], U8, name="hid_s", align_bytes=64)
-        nc.scalar.activation(out=hid_g[1][:], in_=diff[:, :, OH:O].rearrange("p t o -> p o t"), func=ACT.Abs)
-        low = diff[:, :, 0:OH].rearrange("p t o -> p o t")
-        nc.vector.scalar_tensor_tensor(out=hid_g[0][:], in0=low, scalar=-1.0, in1=low, op0=ALU.mult, op1=ALU.max)
-        for h in range(2):
+        nc.scalar.activation(
+            out=hid_g[1][:].rearrange("p (c i) t -> p c t i", i=2),
+            in_=diff[:, :, OH:O].rearrange("p t (c i) -> p c t i", i=2),
+            func=ACT.Abs,
+        )
+        nc.vector.tensor_copy(
+            out=hid_g[0][:].rearrange("p (c i) t -> p c t i", i=4),
+            in_=mag[:].rearrange("p t (c i) -> p c t i", i=4),
+        )
+        for h in (1, 0):
             cols = slice(h * OH, (h + 1) * OH)
             nc.vector.quantize_mx(out=hid_w[:, cols].bitcast(FP8X4), scales=hid_s[:, cols], in_=hid_g[h][:].rearrange("p o t -> p (o t)"))
 
@@ -213,8 +233,8 @@ def tile_picked_tokens_codes_one_boardmixed_outcomes_outmeet_kernel(
             nc.tensor.matmul_mx(out=bank[:], lhsT=w, lhsT_scale=s, rhs=hid_w[:, lo:hi].bitcast(FP8X4), rhs_scale=hid_s[:, lo:hi], start=True, stop=True)
             copy(out=outcome[m, u][:, lo:hi], in_=bank[:])
 
-        second_product(0, 0, 0, OH, 0, nc.scalar.copy)
-        second_product(0, 0, OH, O, 1, nc.scalar.copy)
+        second_product(0, 0, OH, O, 0, nc.scalar.copy)
+        second_product(0, 0, 0, OH, 1, nc.scalar.copy)
         second_product(1, 0, 0, O, 2, nc.vector.tensor_copy)
         second_product(0, 1, 0, O, 3, nc.vector.tensor_copy)
         second_product(1, 1, 0, O, 4, nc.vector.tensor_copy)

@@ -18,6 +18,7 @@ P = 128
 PACK = 4
 HALF = 512
 OH = O // 2
+OQ = O // 4
 FLOPS = 2 * K * R * J + 2 * 2 * R * N * O
 
 
@@ -69,9 +70,8 @@ def tile_picked_tokens_codes_one_boardmixed_outcomes_outmeet_kernel(
         sb_sb = load_by_word(sb, "sb_sb")
 
         board = [keep.tile([P, C], F32, name=f"board{t}") for t in range(PACK)]
-        for t in range(2):
+        for t in range(PACK):
             nc.vector.memset(board[t][:].bitcast(I32), 0)
-            nc.gpsimd.memset(board[t + 2][:].bitcast(I32), 0)
         xs = keep.tile([P, J], U8, name="xs", align_bytes=64)
         nc.vector.tensor_copy(out=xs[:], in_=xs_win[:].indirect(l_xt[:]))
 
@@ -149,11 +149,6 @@ def tile_picked_tokens_codes_one_boardmixed_outcomes_outmeet_kernel(
         first = [keep.tile([P, O], F32, name=f"first{t}") for t in range(PACK)]
         second = [keep.tile([P, O], F32, name=f"second{t}") for t in range(PACK)]
         diff = keep.tile([P, PACK, O], F32, name="diff")
-        mag = keep.tile([P, PACK, OH], BF16, name="mag")
-
-        def magnitude(t):
-            d = diff[:, t, 0:OH]
-            nc.vector.scalar_tensor_tensor(out=mag[:, t, :], in0=d, scalar=-1.0, in1=d, op0=ALU.mult, op1=ALU.max)
 
         def read_second(t):
             nc.scalar.activation(out=second[t][:], in_=board[t][:].indirect(l_b[:]), func=ACT.Copy, scale=sb_sb[:, t : t + 1])
@@ -193,51 +188,43 @@ def tile_picked_tokens_codes_one_boardmixed_outcomes_outmeet_kernel(
             read_second(t)
             read_first(t, 0, O)
         read_second(3)
-        read_first(3, OH, O)
         read_first(3, 0, OH)
-        subtract(0, 0, O)
-        subtract(1, 0, O)
-        magnitude(0)
-        subtract(2, 0, O)
-        magnitude(1)
-        magnitude(2)
-        subtract(3, OH, O)
+        read_first(3, OH, O)
+        for t in range(3):
+            subtract(t, 0, O)
         subtract(3, 0, OH)
-        magnitude(3)
+        subtract(3, OH, O)
 
-        hid_g = [keep.tile([P, OH, PACK], BF16, name=f"hid_g{h}", align_bytes=64) for h in range(2)]
+        hid_g = keep.tile([P, O, PACK], BF16, name="hid_g", align_bytes=64)
         hid_w = keep.tile([P, O], U32, name="hid_w", align_bytes=64)
         hid_s = keep.tile([P, O], U8, name="hid_s", align_bytes=64)
-        nc.scalar.activation(
-            out=hid_g[1][:].rearrange("p (c i) t -> p c t i", i=2),
-            in_=diff[:, :, OH:O].rearrange("p t (c i) -> p c t i", i=2),
-            func=ACT.Abs,
-        )
-        nc.vector.tensor_copy(
-            out=hid_g[0][:].rearrange("p (c i) t -> p c t i", i=4),
-            in_=mag[:].rearrange("p t (c i) -> p c t i", i=4),
-        )
-        for h in (1, 0):
-            cols = slice(h * OH, (h + 1) * OH)
-            nc.vector.quantize_mx(out=hid_w[:, cols].bitcast(FP8X4), scales=hid_s[:, cols], in_=hid_g[h][:].rearrange("p o t -> p (o t)"))
+        woven = diff[:].rearrange("p t o -> p o t")
+        nc.scalar.activation(out=hid_g[:, 0:OH], in_=woven[:, 0:OH], func=ACT.Abs)
+        third = woven[:, OH : OH + OQ]
+        nc.vector.scalar_tensor_tensor(out=hid_g[:, OH : OH + OQ], in0=third, scalar=-1.0, in1=third, op0=ALU.mult, op1=ALU.max)
+        nc.scalar.activation(out=hid_g[:, OH + OQ : O], in_=woven[:, OH + OQ : O], func=ACT.Abs)
+        for lo, hi in ((0, OH), (OH, OH + OQ), (OH + OQ, O)):
+            nc.vector.quantize_mx(out=hid_w[:, lo:hi].bitcast(FP8X4), scales=hid_s[:, lo:hi], in_=hid_g[:, lo:hi].rearrange("p o t -> p (o t)"))
 
         outcome = {(m, u): keep.tile([P, O], F32, name=f"outcome{m}{u}") for m in range(2) for u in range(2)}
 
-        def second_product(m, u, lo, hi, tag, copy):
+        def second_product(m, u, cuts, tag, copy):
+            lo, hi = cuts[0], cuts[-1]
             bank = psum.tile([P, hi - lo], F32, name=f"res{tag}", tag=f"bank{tag}")
             cols = slice(u * P, (u + 1) * P)
             if m == 0:
                 w, s = wb_w[:, 2 * u * P : 2 * (u + 1) * P].bitcast(FP4X4), wb_s[:, cols]
             else:
                 w, s = wo_w[:, cols].bitcast(FP8X4), wo_s[:, cols]
-            nc.tensor.matmul_mx(out=bank[:], lhsT=w, lhsT_scale=s, rhs=hid_w[:, lo:hi].bitcast(FP8X4), rhs_scale=hid_s[:, lo:hi], start=True, stop=True)
+            for a, b in zip(cuts, cuts[1:]):
+                nc.tensor.matmul_mx(out=bank[:, a - lo : b - lo], lhsT=w, lhsT_scale=s, rhs=hid_w[:, a:b].bitcast(FP8X4), rhs_scale=hid_s[:, a:b], start=True, stop=True)
             copy(out=outcome[m, u][:, lo:hi], in_=bank[:])
 
-        second_product(0, 0, OH, O, 0, nc.scalar.copy)
-        second_product(0, 0, 0, OH, 1, nc.scalar.copy)
-        second_product(1, 0, 0, O, 2, nc.vector.tensor_copy)
-        second_product(0, 1, 0, O, 3, nc.vector.tensor_copy)
-        second_product(1, 1, 0, O, 4, nc.vector.tensor_copy)
+        second_product(0, 0, (0, OH), 0, nc.scalar.copy)
+        second_product(0, 0, (OH, OH + OQ, O), 1, nc.scalar.copy)
+        second_product(1, 0, (0, O), 2, nc.vector.tensor_copy)
+        second_product(0, 1, (0, O), 3, nc.vector.tensor_copy)
+        second_product(1, 1, (0, O), 4, nc.vector.tensor_copy)
         for u in range(2):
             p_at = keep.tile([P, U], F32, name=f"p_at{u}")
             q_at = keep.tile([P, U], F32, name=f"q_at{u}")

@@ -181,8 +181,8 @@ def tile_picked_tokens_codes_one_boardmixed_outcomes_outmeet_kernel(
         put_scalar(0, 640, J)
         put_vector(2, 0, J)
         fetch_scalar(3, 0, HALF)
+        fetch_scalar(3, HALF, J)
         put_scalar(3, 0, 384)
-        fetch_vector(3, HALF, J)
         put_vector(3, 384, J)
         for t in range(3):
             read_second(t)
@@ -230,6 +230,8 @@ def tile_picked_tokens_codes_one_boardmixed_outcomes_outmeet_kernel(
             q_at = keep.tile([P, U], F32, name=f"q_at{u}")
             y = keep.tile([P, U], F32, name=f"y{u}")
             nc.scalar.activation(out=p_at[:], in_=outcome[0, u][:].indirect(l_p[:]), func=ACT.Copy, scale=so_sb[u][:])
-            nc.scalar.activation(out=q_at[:], in_=outcome[1, u][:].indirect(l_q[:]), func=ACT.Copy, scale=sp_sb[u][:])
-            nc.vector.tensor_tensor(out=y[:], in0=p_at[:], in1=q_at[:], op=ALU.subtract)
-            nc.sync.dma_start(out[u * P : (u + 1) * P, :], y[:])
+            cuts = (0, U) if u == 0 else (0, U // 2, U)
+            for lo, hi in zip(cuts, cuts[1:]):
+                nc.scalar.activation(out=q_at[:, lo:hi], in_=outcome[1, u][:].indirect(entries(l_q, lo, hi)), func=ACT.Copy, scale=sp_sb[u][:])
+                nc.vector.tensor_tensor(out=y[:, lo:hi], in0=p_at[:, lo:hi], in1=q_at[:, lo:hi], op=ALU.subtract)
+                nc.sync.dma_start(out[u * P : (u + 1) * P, lo:hi], y[:, lo:hi])

from contextlib import ExitStack

import concourse.mybir as mybir

F32 = mybir.dt.float32
BF16 = mybir.dt.bfloat16
I32 = mybir.dt.int32
U32 = mybir.dt.uint32
U16 = mybir.dt.uint16
U8 = mybir.dt.uint8
FP8X4 = mybir.dt.float8_e4m3fn_x4
FP4X4 = mybir.dt.float4_e2m1fn_x4
ACT = mybir.ActivationFunctionType
ALU = mybir.AluOpType

K, J, R, T, F, C, O, N, U = 512, 1024, 512, 2048, 1024, 2048, 512, 256, 256
P = 128
PACK = 4
HALF = 512
OH = O // 2
OQ = O // 4
FLOPS = 2 * K * R * J + 2 * 2 * R * N * O


def tile_picked_tokens_codes_one_boardmixed_outcomes_outmeet_kernel(
    tc, xt_words, xt_scales, ua, ha, sa, sb, wb_words, wb_scales, wo_words, wo_scales, so, sp,
    offs, offs2, offs3, offs4, offs5, offs6, offs7, out,
):
    nc = tc.nc
    with ExitStack() as ctx:
        lists = ctx.enter_context(tc.tile_pool(name="lists", bufs=1))
        keep = ctx.enter_context(tc.tile_pool(name="keep", bufs=1))
        psum = ctx.enter_context(tc.psum_pool(name="psum", bufs=1))

        def load_list(src, name):
            tile = lists.tile([P, src.shape[1]], U16, name=name)
            nc.sync.dma_start(tile[:], src)
            return tile

        def entries(tile, lo, hi):
            return tile[:, lo // 16 : hi // 16]

        def load_by_word(src, name):
            tile = keep.tile([P, PACK], F32, name=name)
            nc.sync.dma_start(tile[:], src.rearrange("(p t) o -> p (t o)", t=PACK))
            return tile

        ha_sb = keep.tile([P, PACK], F32, name="ha_sb")
        nc.scalar.dma_start(ha_sb[:], ha.rearrange("(p t) o -> p (t o)", t=PACK))
        xs_win = keep.tile([P, T], U8, name="xs_win")
        nc.vector.memset(xs_win[:].bitcast(I32), 0)
        for q in range(4):
            nc.scalar.dma_start(xs_win[:].bitcast(I32)[32 * q : 32 * q + 4, :], xt_scales[0].bitcast(I32)[4 * q : 4 * q + 4, :])
        idle = keep.tile([P, 16], F32, name="idle")
        nc.gpsimd.memset(idle[:, 0:1], 0.0)
        nc.scalar.activation(out=idle[:, 8:9], in_=idle[:, 0:1], func=ACT.Copy)
        l_ua = load_list(offs2, "l_ua")
        ua_rows = ua.rearrange("(p t) f -> t p f", t=PACK)
        ua_sb = [keep.tile([P, F], F32, name=f"ua{t}") for t in range(PACK)]
        nc.sync.dma_start(ua_sb[0][:], ua_rows[0])
        l_xt = load_list(offs, "l_xt")
        for t in range(1, PACK):
            nc.sync.dma_start(ua_sb[t][:], ua_rows[t])
        xw_win = keep.tile([P, T], U32, name="xw_win")
        nc.sync.dma_start(xw_win[:].bitcast(I32), xt_words[0].rearrange("p n t -> p (n t)").bitcast(I32))
        l_put = load_list(offs3, "l_put")
        l_a = load_list(offs4, "l_a")
        l_b = load_list(offs5, "l_b")
        sa_sb = load_by_word(sa, "sa_sb")
        sb_sb = load_by_word(sb, "sb_sb")

        board = [keep.tile([P, C], F32, name=f"board{t}") for t in range(PACK)]
        for t in range(PACK):
            nc.vector.memset(board[t][:].bitcast(I32), 0)
        xs = keep.tile([P, J], U8, name="xs", align_bytes=64)
        nc.vector.tensor_copy(out=xs[:], in_=xs_win[:].indirect(l_xt[:]))

        wb_w = keep.tile([P, 2 * N], U8, name="wb_w", align_bytes=64)
        wo_w = keep.tile([P, N], U32, name="wo_w", align_bytes=64)
        wb_s = keep.tile([P, N], U8, name="wb_s", align_bytes=64)
        wo_s = keep.tile([P, N], U8, name="wo_s", align_bytes=64)
        nc.sync.dma_start(wb_w[:].bitcast(I32), wb_words[0].bitcast(I32))
        nc.sync.dma_start(wo_w[:].bitcast(I32), wo_words[0].rearrange("p n t -> p (n t)").bitcast(I32))
        for plane, src in ((wb_s, wb_scales), (wo_s, wo_scales)):
            nc.vector.memset(plane[:].bitcast(I32), 0)
            for q in range(4):
                nc.sync.dma_start(plane[:].bitcast(I32)[32 * q : 32 * q + 4, :], src[0].bitcast(I32)[4 * q : 4 * q + 4, :])
        l_p = load_list(offs6, "l_p")
        l_q = load_list(offs7, "l_q")
        so_sb = [keep.tile([P, 1], F32, name=f"so{u}") for u in range(2)]
        sp_sb = [keep.tile([P, 1], F32, name=f"sp{u}") for u in range(2)]
        for u in range(2):
            nc.sync.dma_start(so_sb[u][:], so[P * u : P * (u + 1), :])
            nc.sync.dma_start(sp_sb[u][:], sp[P * u : P * (u + 1), :])

        wc = keep.tile([P, PACK, R], BF16, name="wc")
        for j in range(PACK):
            nc.scalar.activation(out=wc[:, j, :], in_=ua_sb[j][:].indirect(l_ua[:]), func=ACT.Copy, scale=ha_sb[:, j : j + 1])
        wc_dealt = wc[:].rearrange("p j (m t) -> p t m j", t=PACK)
        wc_w = keep.tile([P, R], U32, name="wc_w", align_bytes=64)
        wc_s = keep.tile([P, R], U8, name="wc_s", align_bytes=64)
        wc_g = keep.tile([P, PACK, P, PACK], BF16, name="wc_g", align_bytes=64)

        def quantize_wc(lo, hi):
            cols = slice(lo * P, hi * P)
            nc.vector.quantize_mx(out=wc_w[:, cols].bitcast(FP8X4), scales=wc_s[:, cols], in_=wc_g[:, lo:hi].rearrange("p t m j -> p (t m j)"))

        nc.vector.tensor_copy(out=wc_g[:, 0], in_=wc_dealt[:, 0])
        nc.scalar.copy(
            out=wc_g[:].rearrange("p t (c i) j -> p c t i j", i=2)[:, :, 1:PACK],
            in_=wc[:].rearrange("p j (c i t) -> p c t i j", i=2, t=PACK)[:, :, 1:PACK],
        )
        xw = keep.tile([P, J], U32, name="xw", align_bytes=64)

        def gather_words(lo, hi):
            nc.vector.tensor_copy(out=xw[:, lo:hi], in_=xw_win[:].indirect(entries(l_xt, lo, hi)))

        gather_words(0, 256)
        quantize_wc(0, 1)
        gather_words(256, HALF)
        quantize_wc(1, PACK)
        gather_words(HALF, J)

        acc = {}
        for t in range(PACK):
            for h in range(2):
                acc[t, h] = psum.tile([P, HALF], F32, name=f"acc{t}{h}", tag=f"bank{2 * t + h}")

        def product(t, lo, hi):
            nc.tensor.matmul_mx(
                out=acc[t, lo // HALF][:, lo % HALF : lo % HALF + hi - lo], lhsT=wc_w[:, t * P : (t + 1) * P].bitcast(FP8X4), lhsT_scale=wc_s[:, t * P : (t + 1) * P],
                rhs=xw[:, lo:hi].bitcast(FP8X4), rhs_scale=xs[:, lo:hi], start=True, stop=True,
            )

        a_sb = [keep.tile([P, J], F32, name=f"a{t}") for t in range(PACK)]

        def fetch_scalar(t, lo, hi):
            nc.scalar.copy(out=a_sb[t][:, lo:hi], in_=acc[t, lo // HALF][:, lo % HALF : lo % HALF + hi - lo])

        def fetch_vector(t, lo, hi):
            nc.vector.tensor_copy(out=a_sb[t][:, lo:hi], in_=acc[t, lo // HALF][:, lo % HALF : lo % HALF + hi - lo])

        def put_scalar(t, lo, hi):
            nc.scalar.activation(out=board[t][:].indirect(entries(l_put, lo, hi)), in_=a_sb[t][:, lo:hi], func=ACT.Copy)

        def put_vector(t, lo, hi):
            nc.vector.tensor_copy(out=board[t][:].indirect(entries(l_put, lo, hi)), in_=a_sb[t][:, lo:hi])

        first = [keep.tile([P, O], F32, name=f"first{t}") for t in range(PACK)]
        second = [keep.tile([P, O], F32, name=f"second{t}") for t in range(PACK)]
        diff = keep.tile([P, PACK, O], F32, name="diff")

        def read_second(t):
            nc.scalar.activation(out=second[t][:], in_=board[t][:].indirect(l_b[:]), func=ACT.Copy, scale=sb_sb[:, t : t + 1])

        def read_first(t, lo, hi):
            nc.scalar.activation(out=first[t][:, lo:hi], in_=board[t][:].indirect(entries(l_a, lo, hi)), func=ACT.Copy, scale=sa_sb[:, t : t + 1])

        def subtract(t, lo, hi):
            nc.vector.tensor_tensor(out=diff[:, t, lo:hi], in0=first[t][:, lo:hi], in1=second[t][:, lo:hi], op=ALU.subtract)

        product(0, 0, 256)
        fetch_scalar(0, 0, 256)
        put_scalar(0, 0, 256)
        product(1, 0, HALF)
        product(0, 256, HALF)
        product(0, HALF, J)
        product(1, HALF, J)
        for t in (2, 3):
            product(t, 0, HALF)
            product(t, HALF, J)
        fetch_vector(1, 0, HALF)
        put_vector(1, 0, HALF)
        fetch_vector(1, HALF, J)
        put_vector(1, HALF, J)
        fetch_scalar(0, 256, HALF)
        fetch_scalar(0, HALF, J)
        put_scalar(0, 256, 640)
        fetch_scalar(2, 0, HALF)
        fetch_scalar(2, HALF, J)
        put_scalar(0, 640, J)
        put_vector(2, 0, J)
        fetch_scalar(3, 0, HALF)
        fetch_scalar(3, HALF, J)
        put_scalar(3, 0, 384)
        put_vector(3, 384, J)
        for t in range(3):
            read_second(t)
            read_first(t, 0, O)
        read_second(3)
        read_first(3, 0, OH)
        read_first(3, OH, O)
        for t in range(3):
            subtract(t, 0, O)
        subtract(3, 0, OH)
        subtract(3, OH, O)

        hid_g = keep.tile([P, O, PACK], BF16, name="hid_g", align_bytes=64)
        hid_w = keep.tile([P, O], U32, name="hid_w", align_bytes=64)
        hid_s = keep.tile([P, O], U8, name="hid_s", align_bytes=64)
        woven = diff[:].rearrange("p t o -> p o t")
        nc.scalar.activation(out=hid_g[:, 0:OH], in_=woven[:, 0:OH], func=ACT.Abs)
        third = woven[:, OH : OH + OQ]
        nc.vector.scalar_tensor_tensor(out=hid_g[:, OH : OH + OQ], in0=third, scalar=-1.0, in1=third, op0=ALU.mult, op1=ALU.max)
        nc.scalar.activation(out=hid_g[:, OH + OQ : O], in_=woven[:, OH + OQ : O], func=ACT.Abs)
        for lo, hi in ((0, OH), (OH, OH + OQ), (OH + OQ, O)):
            nc.vector.quantize_mx(out=hid_w[:, lo:hi].bitcast(FP8X4), scales=hid_s[:, lo:hi], in_=hid_g[:, lo:hi].rearrange("p o t -> p (o t)"))

        outcome = {(m, u): keep.tile([P, O], F32, name=f"outcome{m}{u}") for m in range(2) for u in range(2)}

        def second_product(m, u, cuts, tag, copy):
            lo, hi = cuts[0], cuts[-1]
            bank = psum.tile([P, hi - lo], F32, name=f"res{tag}", tag=f"bank{tag}")
            cols = slice(u * P, (u + 1) * P)
            if m == 0:
                w, s = wb_w[:, 2 * u * P : 2 * (u + 1) * P].bitcast(FP4X4), wb_s[:, cols]
            else:
                w, s = wo_w[:, cols].bitcast(FP8X4), wo_s[:, cols]
            for a, b in zip(cuts, cuts[1:]):
                nc.tensor.matmul_mx(out=bank[:, a - lo : b - lo], lhsT=w, lhsT_scale=s, rhs=hid_w[:, a:b].bitcast(FP8X4), rhs_scale=hid_s[:, a:b], start=True, stop=True)
            copy(out=outcome[m, u][:, lo:hi], in_=bank[:])

        second_product(0, 0, (0, OH), 0, nc.scalar.copy)
        second_product(0, 0, (OH, OH + OQ, O), 1, nc.scalar.copy)
        second_product(1, 0, (0, O), 2, nc.vector.tensor_copy)
        second_product(0, 1, (0, O), 3, nc.vector.tensor_copy)
        second_product(1, 1, (0, O), 4, nc.vector.tensor_copy)
        for u in range(2):
            p_at = keep.tile([P, U], F32, name=f"p_at{u}")
            q_at = keep.tile([P, U], F32, name=f"q_at{u}")
            y = keep.tile([P, U], F32, name=f"y{u}")
            nc.scalar.activation(out=p_at[:], in_=outcome[0, u][:].indirect(l_p[:]), func=ACT.Copy, scale=so_sb[u][:])
            cuts = (0, U) if u == 0 else (0, U // 2, U)
            for lo, hi in zip(cuts, cuts[1:]):
                nc.scalar.activation(out=q_at[:, lo:hi], in_=outcome[1, u][:].indirect(entries(l_q, lo, hi)), func=ACT.Copy, scale=sp_sb[u][:])
                nc.vector.tensor_tensor(out=y[:, lo:hi], in0=p_at[:, lo:hi], in1=q_at[:, lo:hi], op=ALU.subtract)
                nc.sync.dma_start(out[u * P : (u + 1) * P, lo:hi], y[:, lo:hi])
